import numpy as np
import ml_dtypes


def mxq(x, axis, fmt="e4m3"):
    dtype, down = {"e4m3": (ml_dtypes.float8_e4m3fn, 7), "e5m2": (ml_dtypes.float8_e5m2, 14)}[fmt]
    v = np.moveaxis(np.asarray(x, np.float32).astype(ml_dtypes.bfloat16).astype(np.float64), axis, -1)
    blocks = v.reshape(v.shape[:-1] + (-1, 32))
    amax = np.abs(blocks).max(-1, keepdims=True)
    byte = np.maximum(np.where(amax > 0, np.frexp(amax)[1] - 1 + 127, 0) - down, 1)
    scale = np.exp2(byte - 127.0)
    codes = (blocks / scale).astype(np.float32).astype(dtype).astype(np.float64)
    return np.moveaxis((codes * scale).reshape(v.shape), -1, axis)


WIDE = False


def mx_kscale(k):
    if not WIDE:
        return np.ones(k)
    levels = np.array([10, -10, 5, -5, 0])
    if k % 512:
        return np.exp2(np.random.permutation(np.resize(levels, k // 32))).repeat(32)
    a = np.empty((k // 512, 16))
    for p in range(k // 512):
        a[p, :8] = np.random.permutation(np.resize(levels, 8))
        for g in range(8):
            far = levels[np.abs(levels - a[p, g]) >= 10]
            a[p, g + 8] = far[np.random.randint(len(far))]
    return np.exp2(a.ravel()).repeat(32)


def f64(x):
    return np.asarray(x).astype(np.float64)


def striped(idx):
    return np.tile(idx.reshape(-1, 16).T, (8, 1)).astype(np.uint16)


def unstriped(offs):
    return offs[:16].T.reshape(-1).astype(np.int64)


def pack_weight(w):
    k, n = w.shape
    w = f64(np.asarray(w, np.float32).astype(ml_dtypes.bfloat16)).reshape(k // 32, 32, n)
    amax = np.abs(w).max(1)
    byte = np.clip(np.where(amax > 0, np.frexp(amax)[1] - 1 + 127 - 7, 1), 1, 254)
    scaled = (w * np.exp2(127.0 - byte)[:, None, :]).reshape(k, n).astype(np.float32)
    words = np.ascontiguousarray(scaled.reshape(k // 512, 128, 4, n).transpose(0, 1, 3, 2)).astype(ml_dtypes.float8_e4m3fn).view(np.uint8)
    return words, np.ascontiguousarray(byte.astype(np.uint8).reshape(k // 512, 16, n))


def unpack_weight(words, scales):
    g, p, n, _ = words.shape
    vals = np.ascontiguousarray(words).view(ml_dtypes.float8_e4m3fn).astype(np.float64) * np.repeat(np.exp2(scales.astype(np.float64) - 127.0), 8, axis=1)[..., None]
    return vals.transpose(0, 1, 3, 2).reshape(g * 512, n)


K, T, E, C, N = 1536, 512, 4, 256, 128


def by_expert(wq, xq):
    return np.concatenate([wq[e].T @ xq[:, e * C:(e + 1) * C] for e in range(E)], axis=1)


def setup_inputs():
    n = np.random.standard_normal
    s = mx_kscale(K)[:, None]
    first = np.random.permutation(np.repeat(np.arange(E), T // E))
    second = (first + 1 + np.random.permutation(np.repeat(np.arange(E - 1), -(-T // (E - 1)))[:T])) % E
    while np.bincount(second, minlength=E).max() != T // E:
        load = np.bincount(second, minlength=E); hi, lo = int(load.argmax()), int(load.argmin())
        t = np.flatnonzero((second == hi) & (first != lo))[0]; second[t] = lo
    slot_token = np.empty(E * C, np.int64); pos = np.empty((2, T), np.int64); fill = np.zeros(E, np.int64)
    place = np.stack([np.random.permutation(C) for _ in range(E)])
    for r, deal in enumerate((first, second)):
        for t in np.random.permutation(T):
            e = deal[t]; j = e * C + place[e, fill[e]]; fill[e] += 1; slot_token[j] = t; pos[r, t] = j
    g = np.random.uniform(0.2, 0.8, T)
    packed = [pack_weight(m) for m in n((E, K, N)) / np.sqrt(K) / s[None]]
    return {
        "xT": (n((K, T)) * s).astype(np.float32),
        "w_words": np.stack([m[0] for m in packed]),
        "w_scales": np.stack([m[1] for m in packed]),
        "gate": np.stack([np.tile(g, (N, 1)), np.tile(1.0 - g, (N, 1))]).astype(np.float32),
        "offs": striped(slot_token),
        "pos1": striped(pos[0]),
        "pos2": striped(pos[1]),
    }


def reference(xT, w_words, w_scales, gate, offs, pos1, pos2):
    idx = unstriped(offs)
    xq = mxq(f64(xT)[:, idx], 0, "e4m3")
    w = np.stack([unpack_weight(w_words[e], w_scales[e]) for e in range(E)])
    y = by_expert(w, xq)
    return f64(gate[0]) * y[:, unstriped(pos1)] + f64(gate[1]) * y[:, unstriped(pos2)]

@@ -1,0 +1,128 @@
+import concourse.mybir as mybir
+
+K, T, E, C, N = 1536, 512, 4, 256, 128
+P = 128
+KP = 512
+A = K // KP
+S = E * C
+FLOPS = 2 * K * N * S
+
+F32 = mybir.dt.float32
+BF16 = mybir.dt.bfloat16
+I32 = mybir.dt.int32
+U32 = mybir.dt.uint32
+U16 = mybir.dt.uint16
+U8 = mybir.dt.uint8
+X4 = mybir.dt.float8_e4m3fn_x4
+MULT = mybir.AluOpType.mult
+
+WIDE = 1376
+LAST = 704
+V_TOKENS = (336, 96, 0)
+PIECES = ((0, 0, 256), (1, 256, 512), (2, 512, 768), (3, 768, 896), (3, 896, 1024))
+LAST_CUTS = ((0, 512), (512, 768), (768, 896), (896, 1024))
+
+
+def interleaved(grouped, raw, lo, hi):
+    return (
+        grouped[:, lo:hi, :].rearrange("p (c i) t -> p c t i", i=4),
+        raw[:, :, lo:hi].rearrange("p t (c i) -> p c t i", i=4),
+    )
+
+
+def tile_routed_moe_kernel(tc, xT, w_words, w_scales, gate, offs, pos1, pos2, out):
+    nc = tc.nc
+    with (
+        tc.tile_pool(name="keep", bufs=1) as keep,
+        tc.psum_pool(name="psum", bufs=1) as psum,
+    ):
+        lists = keep.tile([P, S // 16], U16, name="lists")
+        p1 = keep.tile([P, T // 16], U16, name="p1")
+        p2 = keep.tile([P, T // 16], U16, name="p2")
+        raw = [keep.tile([P, 4, T], F32, name=f"raw{a}", align_bytes=64) for a in range(A)]
+        grouped = [keep.tile([P, T, 4], BF16, name=f"grouped{a}", align_bytes=64) for a in range(A)]
+        widths = (WIDE, WIDE, LAST)
+        words = [keep.tile([P, widths[a]], I32, name=f"words{a}", align_bytes=64) for a in range(A)]
+        planes = keep.tile([P, WIDE], U8, name="planes", align_bytes=64)
+        slot_words = [keep.tile([P, S], U32, name=f"slot_words{a}", align_bytes=64) for a in range(A)]
+        slot_planes = keep.tile([P, S], U8, name="slot_planes", align_bytes=64)
+        w_codes = keep.tile([P, E * A, 4 * N], U8, name="w_codes", align_bytes=64)
+        w_planes = keep.tile([P, E * A, N], U8, name="w_planes", align_bytes=64)
+        gates = keep.tile([P, 2, T], F32, name="gates", align_bytes=64)
+        y = keep.tile([P, S], F32, name="y", align_bytes=64)
+        first = keep.tile([P, T], F32, name="first", align_bytes=64)
+        second = keep.tile([P, T], F32, name="second", align_bytes=64)
+        result = keep.tile([P, T], F32, name="result", align_bytes=64)
+        warm = keep.tile([P, 2], F32, name="warm")
+        accs = [psum.tile([N, hi - lo], F32, name=f"acc{j}") for j, (e, lo, hi) in enumerate(PIECES)]
+
+        x_rows = xT.rearrange("(a p t) n -> a p t n", p=P, t=4)
+        nc.sync.dma_start(out=raw[0][:], in_=x_rows[0])
+        nc.sync.dma_start(lists[:], offs)
+        for a in range(1, A):
+            nc.sync.dma_start(out=raw[a][:], in_=x_rows[a])
+
+        nc.vector.memset(warm[:], 0.0)
+        nc.scalar.copy(warm[:, 1:2], warm[:, 0:1])
+        nc.vector.memset(w_planes[:].rearrange("p g n -> p (g n)").bitcast(I32), 0)
+        nc.gpsimd.memset(planes[:], 0)
+        for a in range(A):
+            nc.vector.memset(words[a][:, T:], 0)
+
+        nc.sync.dma_start(out=w_codes[:], in_=w_words.rearrange("e a p n r -> p (e a) (n r)"))
+        for q in range(4):
+            nc.sync.dma_start(
+                out=w_planes[32 * q : 32 * q + 4, :, :].bitcast(I32),
+                in_=w_scales[:, :, 4 * q : 4 * q + 4, :].rearrange("e a r n -> r (e a) n").bitcast(I32),
+            )
+        nc.sync.dma_start(p1[:], pos1)
+        nc.sync.dma_start(p2[:], pos2)
+        nc.sync.dma_start(out=gates[:], in_=gate.rearrange("g p t -> p g t"))
+
+        def quantise(a):
+            v = V_TOKENS[a]
+            if v:
+                dst, src = interleaved(grouped[a], raw[a], 0, v)
+                nc.vector.tensor_copy(dst, src)
+            dst, src = interleaved(grouped[a], raw[a], v, T)
+            nc.scalar.copy(dst, src)
+            nc.vector.quantize_mx(
+                out=words[a][:, :T].bitcast(X4),
+                scales=planes[4 * a :, :T],
+                in_=grouped[a][:].rearrange("p n t -> p (n t)"),
+            )
+
+        def multiply(a, j):
+            e, lo, hi = PIECES[j]
+            nc.tensor.matmul_mx(
+                out=accs[j][:],
+                lhsT=w_codes[:, e * A + a, :].bitcast(X4),
+                lhsT_scale=w_planes[:, e * A + a, :],
+                rhs=slot_words[a][:, lo:hi].bitcast(X4),
+                rhs_scale=slot_planes[4 * a :, lo:hi],
+                start=(a == 0),
+                stop=(a == A - 1),
+            )
+
+        for a in range(A - 1):
+            quantise(a)
+            nc.vector.tensor_copy(slot_words[a][:], words[a][:].bitcast(U32).indirect(lists[:]))
+        quantise(A - 1)
+        nc.vector.tensor_copy(slot_planes[:], planes[:].indirect(lists[:]))
+        for a in range(A - 1):
+            for j in range(len(PIECES)):
+                multiply(a, j)
+        for lo, hi in LAST_CUTS:
+            nc.vector.tensor_copy(
+                slot_words[A - 1][:, lo:hi],
+                words[A - 1][:].bitcast(U32).indirect(lists[:, lo // 16 : hi // 16]),
+            )
+            for j, (e, piece_lo, piece_hi) in enumerate(PIECES):
+                if lo <= piece_lo and piece_hi <= hi:
+                    multiply(A - 1, j)
+                    nc.scalar.copy(y[:, piece_lo:piece_hi], accs[j][:])
+
+        nc.vector.tensor_tensor(first[:], y[:].indirect(p1[:]), gates[:, 0, :], MULT)
+        nc.vector.tensor_tensor(second[:], y[:].indirect(p2[:]), gates[:, 1, :], MULT)
+        nc.vector.tensor_add(result[:], first[:], second[:])
+        nc.sync.dma_start(out=out, in_=result[:])

@@ -18,9 +18,10 @@ MULT = mybir.AluOpType.mult
 
 WIDE = 1376
 LAST = 704
-V_TOKENS = (336, 96, 0)
+V_TOKENS = (336, 64, 64)
 PIECES = ((0, 0, 256), (1, 256, 512), (2, 512, 768), (3, 768, 896), (3, 896, 1024))
-LAST_CUTS = ((0, 512), (512, 768), (768, 896), (896, 1024))
+LAST_CUTS = ((0, 256), (256, 512), (512, 768), (768, 896), (896, 1024))
+HALVES = ((0, 256), (256, 512))
 
 
 def interleaved(grouped, raw, lo, hi):
@@ -79,18 +80,24 @@ def tile_routed_moe_kernel(tc, xT, w_words, w_scales, gate, offs, pos1, pos2, ou
         nc.sync.dma_start(p2[:], pos2)
         nc.sync.dma_start(out=gates[:], in_=gate.rearrange("g p t -> p g t"))
 
-        def quantise(a):
-            v = V_TOKENS[a]
-            if v:
-                dst, src = interleaved(grouped[a], raw[a], 0, v)
-                nc.vector.tensor_copy(dst, src)
-            dst, src = interleaved(grouped[a], raw[a], v, T)
-            nc.scalar.copy(dst, src)
+        def cast(a, copy, lo, hi):
+            dst, src = interleaved(grouped[a], raw[a], lo, hi)
+            copy(dst, src)
+
+        def quantise(a, lo, hi):
             nc.vector.quantize_mx(
-                out=words[a][:, :T].bitcast(X4),
-                scales=planes[4 * a :, :T],
-                in_=grouped[a][:].rearrange("p n t -> p (n t)"),
+                out=words[a][:, lo:hi].bitcast(X4),
+                scales=planes[4 * a :, lo:hi],
+                in_=grouped[a][:, lo:hi, :].rearrange("p n t -> p (n t)"),
             )
+
+        def fetch_words(a, lo, hi):
+            nc.vector.tensor_copy(
+                slot_words[a][:, lo:hi], words[a][:].bitcast(U32).indirect(lists[:, lo // 16 : hi // 16])
+            )
+
+        def fetch_planes(lo, hi):
+            nc.vector.tensor_copy(slot_planes[:, lo:hi], planes[:].indirect(lists[:, lo // 16 : hi // 16]))
 
         def multiply(a, j):
             e, lo, hi = PIECES[j]
@@ -104,25 +111,35 @@ def tile_routed_moe_kernel(tc, xT, w_words, w_scales, gate, offs, pos1, pos2, ou
                 stop=(a == A - 1),
             )
 
-        for a in range(A - 1):
-            quantise(a)
-            nc.vector.tensor_copy(slot_words[a][:], words[a][:].bitcast(U32).indirect(lists[:]))
-        quantise(A - 1)
-        nc.vector.tensor_copy(slot_planes[:], planes[:].indirect(lists[:]))
-        for a in range(A - 1):
-            for j in range(len(PIECES)):
+        v, s = nc.vector.tensor_copy, nc.scalar.copy
+        cast(0, s, V_TOKENS[0], T)
+        cast(0, v, 0, 256)
+        cast(0, v, 256, V_TOKENS[0])
+        quantise(0, 0, 256)
+        quantise(0, 256, T)
+        fetch_words(0, 0, S)
+        cast(1, s, V_TOKENS[1], T)
+        cast(1, v, 0, V_TOKENS[1])
+        quantise(1, 256, T)
+        quantise(1, 0, 256)
+        cast(2, s, V_TOKENS[2], T)
+        cast(2, v, 0, V_TOKENS[2])
+        fetch_words(1, 0, 768)
+        quantise(2, 0, T)
+        fetch_words(1, 768, S)
+        for lo, hi in HALVES:
+            fetch_planes(2 * lo, 2 * hi)
+        for j in range(len(PIECES)):
+            for a in range(A - 1):
                 multiply(a, j)
-        for lo, hi in LAST_CUTS:
-            nc.vector.tensor_copy(
-                slot_words[A - 1][:, lo:hi],
-                words[A - 1][:].bitcast(U32).indirect(lists[:, lo // 16 : hi // 16]),
-            )
-            for j, (e, piece_lo, piece_hi) in enumerate(PIECES):
-                if lo <= piece_lo and piece_hi <= hi:
-                    multiply(A - 1, j)
-                    nc.scalar.copy(y[:, piece_lo:piece_hi], accs[j][:])
+        for j, (lo, hi) in enumerate(LAST_CUTS):
+            fetch_words(2, lo, hi)
+            multiply(2, j)
+            nc.scalar.copy(y[:, lo:hi], accs[j][:])
 
         nc.vector.tensor_tensor(first[:], y[:].indirect(p1[:]), gates[:, 0, :], MULT)
-        nc.vector.tensor_tensor(second[:], y[:].indirect(p2[:]), gates[:, 1, :], MULT)
-        nc.vector.tensor_add(result[:], first[:], second[:])
-        nc.sync.dma_start(out=out, in_=result[:])
+        for lo, hi in HALVES:
+            nc.vector.tensor_tensor(second[:, lo:hi], y[:].indirect(p2[:, lo // 16 : hi // 16]), gates[:, 1, lo:hi], MULT)
+        for lo, hi in HALVES:
+            nc.vector.tensor_add(result[:, lo:hi], first[:, lo:hi], second[:, lo:hi])
+            nc.sync.dma_start(out=out[:, lo:hi], in_=result[:, lo:hi])

@@ -18,10 +18,12 @@ MULT = mybir.AluOpType.mult
 
 WIDE = 1376
 LAST = 704
-V_TOKENS = (336, 64, 64)
+V_TOKENS = (336,)
 PIECES = ((0, 0, 256), (1, 256, 512), (2, 512, 768), (3, 768, 896), (3, 896, 1024))
 LAST_CUTS = ((0, 256), (256, 512), (512, 768), (768, 896), (896, 1024))
-HALVES = ((0, 256), (256, 512))
+PLANE_CUTS = ((0, 512), (512, 1024))
+END_CUTS = ((0, 384), (384, 512))
+TOKEN_HALVES = ((0, 256), (256, 512))
 
 
 def interleaved(grouped, raw, lo, hi):
@@ -42,7 +44,7 @@ def tile_routed_moe_kernel(tc, xT, w_words, w_scales, gate, offs, pos1, pos2, ou
         p2 = keep.tile([P, T // 16], U16, name="p2")
         raw = [keep.tile([P, 4, T], F32, name=f"raw{a}", align_bytes=64) for a in range(A)]
         grouped = [keep.tile([P, T, 4], BF16, name=f"grouped{a}", align_bytes=64) for a in range(A)]
-        widths = (WIDE, WIDE, LAST)
+        widths = (WIDE, 1024, LAST)
         words = [keep.tile([P, widths[a]], I32, name=f"words{a}", align_bytes=64) for a in range(A)]
         planes = keep.tile([P, WIDE], U8, name="planes", align_bytes=64)
         slot_words = [keep.tile([P, S], U32, name=f"slot_words{a}", align_bytes=64) for a in range(A)]
@@ -61,14 +63,13 @@ def tile_routed_moe_kernel(tc, xT, w_words, w_scales, gate, offs, pos1, pos2, ou
         nc.sync.dma_start(out=raw[0][:], in_=x_rows[0])
         nc.sync.dma_start(lists[:], offs)
         for a in range(1, A):
-            nc.sync.dma_start(out=raw[a][:], in_=x_rows[a])
+            for lo, hi in TOKEN_HALVES:
+                nc.sync.dma_start(out=raw[a][:, :, lo:hi], in_=x_rows[a][:, :, lo:hi])
 
         nc.vector.memset(warm[:], 0.0)
         nc.scalar.copy(warm[:, 1:2], warm[:, 0:1])
         nc.vector.memset(w_planes[:].rearrange("p g n -> p (g n)").bitcast(I32), 0)
-        nc.gpsimd.memset(planes[:], 0)
-        for a in range(A):
-            nc.vector.memset(words[a][:, T:], 0)
+        nc.gpsimd.memset(planes[:, :T], 0)
 
         nc.sync.dma_start(out=w_codes[:], in_=w_words.rearrange("e a p n r -> p (e a) (n r)"))
         for q in range(4):
@@ -118,17 +119,19 @@ def tile_routed_moe_kernel(tc, xT, w_words, w_scales, gate, offs, pos1, pos2, ou
         quantise(0, 0, 256)
         quantise(0, 256, T)
         fetch_words(0, 0, S)
-        cast(1, s, V_TOKENS[1], T)
-        cast(1, v, 0, V_TOKENS[1])
-        quantise(1, 256, T)
+        for lo, hi in TOKEN_HALVES:
+            cast(1, s, lo, hi)
         quantise(1, 0, 256)
-        cast(2, s, V_TOKENS[2], T)
-        cast(2, v, 0, V_TOKENS[2])
+        quantise(1, 256, T)
+        for lo, hi in TOKEN_HALVES:
+            cast(2, s, lo, hi)
         fetch_words(1, 0, 768)
-        quantise(2, 0, T)
-        fetch_words(1, 768, S)
-        for lo, hi in HALVES:
-            fetch_planes(2 * lo, 2 * hi)
+        quantise(2, 0, 256)
+        fetch_words(1, 768, 896)
+        quantise(2, 256, T)
+        fetch_words(1, 896, S)
+        for lo, hi in PLANE_CUTS:
+            fetch_planes(lo, hi)
         for j in range(len(PIECES)):
             for a in range(A - 1):
                 multiply(a, j)
@@ -138,8 +141,8 @@ def tile_routed_moe_kernel(tc, xT, w_words, w_scales, gate, offs, pos1, pos2, ou
             nc.scalar.copy(y[:, lo:hi], accs[j][:])
 
         nc.vector.tensor_tensor(first[:], y[:].indirect(p1[:]), gates[:, 0, :], MULT)
-        for lo, hi in HALVES:
+        for lo, hi in END_CUTS:
             nc.vector.tensor_tensor(second[:, lo:hi], y[:].indirect(p2[:, lo // 16 : hi // 16]), gates[:, 1, lo:hi], MULT)
-        for lo, hi in HALVES:
+        for lo, hi in END_CUTS:
             nc.vector.tensor_add(result[:, lo:hi], first[:, lo:hi], second[:, lo:hi])
             nc.sync.dma_start(out=out[:, lo:hi], in_=result[:, lo:hi])

@@ -71,12 +71,12 @@ def tile_routed_moe_kernel(tc, xT, w_words, w_scales, gate, offs, pos1, pos2, ou
         nc.vector.memset(w_planes[:].rearrange("p g n -> p (g n)").bitcast(I32), 0)
         nc.gpsimd.memset(planes[:, :T], 0)
 
-        nc.sync.dma_start(out=w_codes[:], in_=w_words.rearrange("e a p n r -> p (e a) (n r)"))
         for q in range(4):
             nc.sync.dma_start(
                 out=w_planes[32 * q : 32 * q + 4, :, :].bitcast(I32),
                 in_=w_scales[:, :, 4 * q : 4 * q + 4, :].rearrange("e a r n -> r (e a) n").bitcast(I32),
             )
+        nc.sync.dma_start(out=w_codes[:], in_=w_words.rearrange("e a p n r -> p (e a) (n r)"))
         nc.sync.dma_start(p1[:], pos1)
         nc.sync.dma_start(p2[:], pos2)
         nc.sync.dma_start(out=gates[:], in_=gate.rearrange("g p t -> p g t"))

import concourse.mybir as mybir

K, T, E, C, N = 1536, 512, 4, 256, 128
P = 128
KP = 512
A = K // KP
S = E * C
FLOPS = 2 * K * N * S

F32 = mybir.dt.float32
BF16 = mybir.dt.bfloat16
I32 = mybir.dt.int32
U32 = mybir.dt.uint32
U16 = mybir.dt.uint16
U8 = mybir.dt.uint8
X4 = mybir.dt.float8_e4m3fn_x4
MULT = mybir.AluOpType.mult

WIDE = 1376
LAST = 704
V_TOKENS = (336,)
PIECES = ((0, 0, 256), (1, 256, 512), (2, 512, 768), (3, 768, 896), (3, 896, 1024))
LAST_CUTS = ((0, 256), (256, 512), (512, 768), (768, 896), (896, 1024))
PLANE_CUTS = ((0, 512), (512, 1024))
END_CUTS = ((0, 384), (384, 512))
TOKEN_HALVES = ((0, 256), (256, 512))


def interleaved(grouped, raw, lo, hi):
    return (
        grouped[:, lo:hi, :].rearrange("p (c i) t -> p c t i", i=4),
        raw[:, :, lo:hi].rearrange("p t (c i) -> p c t i", i=4),
    )


def tile_routed_moe_kernel(tc, xT, w_words, w_scales, gate, offs, pos1, pos2, out):
    nc = tc.nc
    with (
        tc.tile_pool(name="keep", bufs=1) as keep,
        tc.psum_pool(name="psum", bufs=1) as psum,
    ):
        lists = keep.tile([P, S // 16], U16, name="lists")
        p1 = keep.tile([P, T // 16], U16, name="p1")
        p2 = keep.tile([P, T // 16], U16, name="p2")
        raw = [keep.tile([P, 4, T], F32, name=f"raw{a}", align_bytes=64) for a in range(A)]
        grouped = [keep.tile([P, T, 4], BF16, name=f"grouped{a}", align_bytes=64) for a in range(A)]
        widths = (WIDE, 1024, LAST)
        words = [keep.tile([P, widths[a]], I32, name=f"words{a}", align_bytes=64) for a in range(A)]
        planes = keep.tile([P, WIDE], U8, name="planes", align_bytes=64)
        slot_words = [keep.tile([P, S], U32, name=f"slot_words{a}", align_bytes=64) for a in range(A)]
        slot_planes = keep.tile([P, S], U8, name="slot_planes", align_bytes=64)
        w_codes = keep.tile([P, E * A, 4 * N], U8, name="w_codes", align_bytes=64)
        w_planes = keep.tile([P, E * A, N], U8, name="w_planes", align_bytes=64)
        gates = keep.tile([P, 2, T], F32, name="gates", align_bytes=64)
        y = keep.tile([P, S], F32, name="y", align_bytes=64)
        first = keep.tile([P, T], F32, name="first", align_bytes=64)
        second = keep.tile([P, T], F32, name="second", align_bytes=64)
        result = keep.tile([P, T], F32, name="result", align_bytes=64)
        warm = keep.tile([P, 2], F32, name="warm")
        accs = [psum.tile([N, hi - lo], F32, name=f"acc{j}") for j, (e, lo, hi) in enumerate(PIECES)]

        x_rows = xT.rearrange("(a p t) n -> a p t n", p=P, t=4)
        nc.sync.dma_start(out=raw[0][:], in_=x_rows[0])
        nc.sync.dma_start(lists[:], offs)
        for a in range(1, A):
            for lo, hi in TOKEN_HALVES:
                nc.sync.dma_start(out=raw[a][:, :, lo:hi], in_=x_rows[a][:, :, lo:hi])

        nc.vector.memset(warm[:], 0.0)
        nc.scalar.copy(warm[:, 1:2], warm[:, 0:1])
        nc.vector.memset(w_planes[:].rearrange("p g n -> p (g n)").bitcast(I32), 0)
        nc.gpsimd.memset(planes[:, :T], 0)

        for q in range(4):
            nc.sync.dma_start(
                out=w_planes[32 * q : 32 * q + 4, :, :].bitcast(I32),
                in_=w_scales[:, :, 4 * q : 4 * q + 4, :].rearrange("e a r n -> r (e a) n").bitcast(I32),
            )
        nc.sync.dma_start(out=w_codes[:], in_=w_words.rearrange("e a p n r -> p (e a) (n r)"))
        nc.sync.dma_start(p1[:], pos1)
        nc.sync.dma_start(p2[:], pos2)
        nc.sync.dma_start(out=gates[:], in_=gate.rearrange("g p t -> p g t"))

        def cast(a, copy, lo, hi):
            dst, src = interleaved(grouped[a], raw[a], lo, hi)
            copy(dst, src)

        def quantise(a, lo, hi):
            nc.vector.quantize_mx(
                out=words[a][:, lo:hi].bitcast(X4),
                scales=planes[4 * a :, lo:hi],
                in_=grouped[a][:, lo:hi, :].rearrange("p n t -> p (n t)"),
            )

        def fetch_words(a, lo, hi):
            nc.vector.tensor_copy(
                slot_words[a][:, lo:hi], words[a][:].bitcast(U32).indirect(lists[:, lo // 16 : hi // 16])
            )

        def fetch_planes(lo, hi):
            nc.vector.tensor_copy(slot_planes[:, lo:hi], planes[:].indirect(lists[:, lo // 16 : hi // 16]))

        def multiply(a, j):
            e, lo, hi = PIECES[j]
            nc.tensor.matmul_mx(
                out=accs[j][:],
                lhsT=w_codes[:, e * A + a, :].bitcast(X4),
                lhsT_scale=w_planes[:, e * A + a, :],
                rhs=slot_words[a][:, lo:hi].bitcast(X4),
                rhs_scale=slot_planes[4 * a :, lo:hi],
                start=(a == 0),
                stop=(a == A - 1),
            )

        v, s = nc.vector.tensor_copy, nc.scalar.copy
        cast(0, s, V_TOKENS[0], T)
        cast(0, v, 0, 256)
        cast(0, v, 256, V_TOKENS[0])
        quantise(0, 0, 256)
        quantise(0, 256, T)
        fetch_words(0, 0, S)
        for lo, hi in TOKEN_HALVES:
            cast(1, s, lo, hi)
        quantise(1, 0, 256)
        quantise(1, 256, T)
        for lo, hi in TOKEN_HALVES:
            cast(2, s, lo, hi)
        fetch_words(1, 0, 768)
        quantise(2, 0, 256)
        fetch_words(1, 768, 896)
        quantise(2, 256, T)
        fetch_words(1, 896, S)
        for lo, hi in PLANE_CUTS:
            fetch_planes(lo, hi)
        for j in range(len(PIECES)):
            for a in range(A - 1):
                multiply(a, j)
        for j, (lo, hi) in enumerate(LAST_CUTS):
            fetch_words(2, lo, hi)
            multiply(2, j)
            nc.scalar.copy(y[:, lo:hi], accs[j][:])

        nc.vector.tensor_tensor(first[:], y[:].indirect(p1[:]), gates[:, 0, :], MULT)
        for lo, hi in END_CUTS:
            nc.vector.tensor_tensor(second[:, lo:hi], y[:].indirect(p2[:, lo // 16 : hi // 16]), gates[:, 1, lo:hi], MULT)
        for lo, hi in END_CUTS:
            nc.vector.tensor_add(result[:, lo:hi], first[:, lo:hi], second[:, lo:hi])
            nc.sync.dma_start(out=out[:, lo:hi], in_=result[:, lo:hi])
